import numpy as np
import ml_dtypes


def mxq(x, axis, fmt="e4m3"):
    dtype, down = {"e4m3": (ml_dtypes.float8_e4m3fn, 7), "e5m2": (ml_dtypes.float8_e5m2, 14)}[fmt]
    v = np.moveaxis(np.asarray(x, np.float32).astype(ml_dtypes.bfloat16).astype(np.float64), axis, -1)
    blocks = v.reshape(v.shape[:-1] + (-1, 32))
    amax = np.abs(blocks).max(-1, keepdims=True)
    byte = np.maximum(np.where(amax > 0, np.frexp(amax)[1] - 1 + 127, 0) - down, 1)
    scale = np.exp2(byte - 127.0)
    codes = (blocks / scale).astype(np.float32).astype(dtype).astype(np.float64)
    return np.moveaxis((codes * scale).reshape(v.shape), -1, axis)


WIDE = False


def mx_kscale(k):
    if not WIDE:
        return np.ones(k)
    levels = np.array([10, -10, 5, -5, 0])
    if k % 512:
        return np.exp2(np.random.permutation(np.resize(levels, k // 32))).repeat(32)
    a = np.empty((k // 512, 16))
    for p in range(k // 512):
        a[p, :8] = np.random.permutation(np.resize(levels, 8))
        for g in range(8):
            far = levels[np.abs(levels - a[p, g]) >= 10]
            a[p, g + 8] = far[np.random.randint(len(far))]
    return np.exp2(a.ravel()).repeat(32)


def f64(x):
    return np.asarray(x).astype(np.float64)


def striped8(idx):
    return np.concatenate([v.reshape(-1, 16).T for v in idx]).astype(np.uint16)


def unstriped8(offs):
    return np.stack([offs[16 * g:16 * g + 16].T.reshape(-1) for g in range(8)]).astype(np.int64)


E2M1 = np.array([0.0, 0.5, 1.0, 1.5, 2.0, 3.0, 4.0, 6.0, -0.0, -0.5, -1.0, -1.5, -2.0, -3.0, -4.0, -6.0])


def pack_weight(w, fmt):
    k, n = w.shape
    w = f64(np.asarray(w, np.float32).astype(ml_dtypes.bfloat16)).reshape(k // 32, 32, n)
    amax = np.abs(w).max(1)
    if fmt == "e4m3":
        byte = np.frexp(amax)[1] - 1 + 127 - 7
    else:
        mant, ex = np.frexp(amax / 6.0)
        byte = np.where(mant > 0.5, ex, ex - 1) + 127
    byte = np.clip(np.where(amax > 0, byte, 1), 1, 254)
    scaled = (w * np.exp2(127.0 - byte)[:, None, :]).reshape(k, n).astype(np.float32)
    by_word = np.ascontiguousarray(scaled.reshape(k // 512, 128, 4, n).transpose(0, 1, 3, 2))
    if fmt == "e4m3":
        words = by_word.astype(ml_dtypes.float8_e4m3fn).view(np.uint8)
    else:
        c = by_word.astype(ml_dtypes.float4_e2m1fn).view(np.uint8) & 0xF
        words = (c[..., 0::2] | (c[..., 1::2] << 4)).reshape(k // 512, 128, 2 * n)
    return np.ascontiguousarray(words), np.ascontiguousarray(byte.astype(np.uint8).reshape(k // 512, 16, n))


def unpack_weight(words, scales, fmt):
    g, _, n = scales.shape
    words = np.ascontiguousarray(words).reshape(g, 128, n, -1)
    if fmt == "e4m3":
        vals = words.view(ml_dtypes.float8_e4m3fn).astype(np.float64)
    else:
        nib = np.empty((g, 128, n, 4), np.uint8)
        nib[..., 0::2] = words & 0xF
        nib[..., 1::2] = words >> 4
        vals = E2M1[nib]
    vals = vals * np.repeat(np.exp2(scales.astype(np.float64) - 127.0), 8, axis=1)[..., None]
    return vals.transpose(0, 1, 3, 2).reshape(g * 512, n)


def gelu(v):
    return 0.5 * v * (1.0 + np.tanh(np.sqrt(2.0 / np.pi) * (v + 0.044715 * v**3)))


K, M, T, S = 1024, 128, 1024, 512


def setup_inputs():
    n = np.random.standard_normal
    s = mx_kscale(K)[:, None]
    w = n((K, M)) / np.sqrt(K) / s
    w4 = pack_weight(w, "e2m1")
    rest = w - unpack_weight(*w4, "e2m1")
    p_r8 = pack_weight(rest, "e4m3")
    return {
        "xT": (n((K, T)) * s).astype(np.float32),
        "w4_words": w4[0],
        "w4_scales": w4[1],
        "r8_words": p_r8[0],
        "r8_scales": p_r8[1],
        "wgt": np.repeat(np.random.uniform(0.5, 2.0, (8, S)), 16, axis=0).astype(np.float32),
        "b": (0.3 * n(128)).astype(np.float32),
        "wgo": np.repeat(np.random.uniform(0.5, 2.0, (8, S)), 16, axis=0).astype(np.float32),
        "offs": striped8(np.stack([np.random.permutation(T)[:S] for _ in range(8)])),
        "offs2": striped8(np.stack([np.random.permutation(T)[:S] for _ in range(8)])),
    }


def reference(xT, w4_words, w4_scales, r8_words, r8_scales, wgt, b, wgo, offs, offs2):
    idx = unstriped8(offs)
    group = np.arange(K) % 512 // 64
    xg = f64(wgt)[np.arange(K) // 4 % 128] * f64(xT)[np.arange(K)[:, None], idx[group]]
    xT_ = mxq(xg, 0, "e4m3")
    w4_ = unpack_weight(w4_words, w4_scales, "e2m1")
    r8_ = unpack_weight(r8_words, r8_scales, "e4m3")
    y = w4_.T @ xT_ + r8_.T @ xT_
    place = unstriped8(offs2)[np.arange(M) % 128 // 16]
    out = np.zeros((M, T))
    out[np.arange(M)[:, None], place] = f64(wgo)[np.arange(M) % 128] * (gelu(y + f64(b)[:, None]))
    return out

@@ -1,0 +1,177 @@
+from contextlib import ExitStack
+
+import concourse.mybir as mybir
+
+FLOPS = 268435456
+
+F32 = mybir.dt.float32
+BF16 = mybir.dt.bfloat16
+U8 = mybir.dt.uint8
+U16 = mybir.dt.uint16
+U32 = mybir.dt.uint32
+I32 = mybir.dt.int32
+E4M3 = mybir.dt.float8_e4m3fn_x4
+E2M1 = mybir.dt.float4_e2m1fn_x4
+
+MULT = mybir.AluOpType.mult
+COPY = mybir.ActivationFunctionType.Copy
+GELU = mybir.ActivationFunctionType.Gelu_apprx_tanh
+
+P = 128
+T = 1024
+S = 512
+H = 256
+NQ = 128
+PASSES = 2
+PACK = 4
+OC = H // 16
+
+
+def tile_list_hboth_gelu_kernel(
+    tc, xT, w4_words, w4_scales, r8_words, r8_scales, wgt, b, wgo, offs, offs2, out
+):
+    nc = tc.nc
+    with ExitStack() as ctx:
+        keep = ctx.enter_context(tc.tile_pool(name="keep", bufs=1))
+        psum = ctx.enter_context(tc.psum_pool(name="psum", bufs=1))
+
+        offs_t = keep.tile([P, S // 16], U16, name="offs_t")
+        offs2_t = keep.tile([P, S // 16], U16, name="offs2_t")
+        wgt_h = [keep.tile([P, H], F32, name="wgt%d" % h, align_bytes=64) for h in range(2)]
+        wgo_t = keep.tile([P, S], F32, name="wgo_t", align_bytes=64)
+        b_t = keep.tile([P, 1], F32, name="b_t")
+        dummy = keep.tile([P, 1], F32, name="dummy")
+        w4_t = keep.tile([P, PASSES, 2 * P], U8, name="w4_t", align_bytes=64)
+        r8_t = keep.tile([P, PASSES, P * PACK], U8, name="r8_t", align_bytes=64)
+        sc_t = keep.tile([P, 2 * PASSES * P], U8, name="sc_t", align_bytes=64)
+        out_t = keep.tile([P, T], F32, name="out_t", align_bytes=64)
+        planes = [
+            [keep.tile([P, T], F32, name="x%d%d" % (a, i), align_bytes=64) for i in range(PACK)]
+            for a in range(PASSES)
+        ]
+
+        nc.vector.memset(dummy[:], 0.0)
+        nc.vector.memset(sc_t[:].bitcast(I32), 0)
+        nc.vector.memset(out_t[:], 0.0)
+        warm = keep.tile([P, 1], F32, name="warm")
+        nc.scalar.activation(warm[:], dummy[:], GELU)
+
+        x_view = xT.rearrange("(a p i) t -> a i p t", a=PASSES, p=P, i=PACK)
+        nc.sync.dma_start(out=offs_t[:], in_=offs)
+        nc.scalar.dma_start(out=wgt_h[0][:], in_=wgt[:, 0:H])
+        nc.sync.dma_start(out=planes[0][0][:], in_=x_view[0, 0])
+        nc.sync.dma_start(out=wgt_h[1][:], in_=wgt[:, H:S])
+        for n in range(1, 4):
+            nc.sync.dma_start(out=planes[n // PACK][n % PACK][:], in_=x_view[n // PACK, n % PACK])
+        for which, scales in enumerate((w4_scales, r8_scales)):
+            cols = slice(which * PASSES * P, (which + 1) * PASSES * P)
+            queue = (nc.gpsimd, nc.scalar)[which]
+            for q in range(4):
+                queue.dma_start(
+                    out=sc_t[32 * q : 32 * q + 4, cols].rearrange("r (a n) -> r a n", a=PASSES).bitcast(I32),
+                    in_=scales[:, 4 * q : 4 * q + 4, :].rearrange("a r n -> r a n").bitcast(I32),
+                )
+        for n in range(4, PASSES * PACK):
+            if n == 6:
+                nc.sync.dma_start(out=offs2_t[:], in_=offs2)
+            nc.sync.dma_start(out=planes[n // PACK][n % PACK][:], in_=x_view[n // PACK, n % PACK])
+        nc.sync.dma_start(out=b_t[:], in_=b.rearrange("(p o) -> p o", o=1))
+        nc.sync.dma_start(
+            out=r8_t[:].bitcast(I32), in_=r8_words.rearrange("a p n i -> p a (n i)").bitcast(I32)
+        )
+        nc.sync.dma_start(out=w4_t[:].bitcast(I32), in_=w4_words.rearrange("a p n -> p a n").bitcast(I32))
+        nc.sync.dma_start(out=wgo_t[:], in_=wgo)
+
+        acc = [psum.tile([P, NQ], F32, name="acc%d" % q) for q in range(4)]
+        val = [keep.tile([P, H], F32, name="val%d" % h, align_bytes=64) for h in range(2)]
+
+        def gather(g, a, i, j0, j1):
+            h = j0 // H
+            nc.vector.tensor_tensor(
+                g[:, i, j0 - h * H : j1 - h * H],
+                planes[a][i][:].indirect(offs_t[:, j0 // 16 : j1 // 16]),
+                wgt_h[h][:, j0 - h * H : j1 - h * H],
+                MULT,
+            )
+
+        def interleave(g, a, j0, j1, on_vector):
+            h = j0 // H
+            xb = keep.tile([P, (j1 - j0) * PACK], BF16, name="xb%d_%d" % (a, j0), align_bytes=64)
+            dst = xb[:].rearrange("p (c i t) -> p c t i", i=4, t=PACK)
+            src = g[:, :, j0 - h * H : j1 - h * H].rearrange("p t (c i) -> p c t i", i=4)
+            if on_vector:
+                nc.vector.tensor_copy(dst, src)
+            else:
+                nc.scalar.activation(dst, src, COPY)
+            return xb
+
+        def quantise(xb, a, j0, j1):
+            codes = keep.tile([P, j1 - j0], U32, name="codes%d_%d" % (a, j0), align_bytes=64)
+            scales = keep.tile([P, j1 - j0], U8, name="scales%d_%d" % (a, j0), align_bytes=64)
+            nc.vector.quantize_mx(out=codes[:].bitcast(E4M3), scales=scales[:], in_=xb[:])
+            return codes, scales
+
+        def multiply(a, j0, j1, codes, scales):
+            for j in range(j0, j1, NQ):
+                cols = slice(j - j0, j - j0 + NQ)
+                nc.tensor.matmul_mx(
+                    out=acc[j // NQ][:],
+                    lhsT=w4_t[:, a, :].bitcast(E2M1),
+                    lhsT_scale=sc_t[:, a * P : (a + 1) * P],
+                    rhs=codes[:, cols].bitcast(E4M3),
+                    rhs_scale=scales[:, cols],
+                    start=(a == 0),
+                    stop=False,
+                )
+                nc.tensor.matmul_mx(
+                    out=acc[j // NQ][:],
+                    lhsT=r8_t[:, a, :].bitcast(E4M3),
+                    lhsT_scale=sc_t[:, (PASSES + a) * P : (PASSES + a + 1) * P],
+                    rhs=codes[:, cols].bitcast(E4M3),
+                    rhs_scale=scales[:, cols],
+                    start=False,
+                    stop=(a == PASSES - 1),
+                )
+
+        def gelu(h):
+            for s in range(2):
+                nc.scalar.activation(
+                    val[h][:, s * NQ : (s + 1) * NQ], acc[2 * h + s][:], GELU, bias=b_t[:, 0:1]
+                )
+
+        def scatter(h):
+            nc.vector.tensor_tensor(
+                out_t[:].indirect(offs2_t[:, h * OC : (h + 1) * OC]),
+                val[h][:],
+                wgo_t[:, h * H : (h + 1) * H],
+                MULT,
+            )
+
+        g = {
+            (h, a): keep.tile([P, PACK, H], F32, name="g%d%d" % (h, a), align_bytes=64)
+            for h in range(2)
+            for a in range(PASSES)
+        }
+        for a in range(PASSES):
+            for i in range(PACK):
+                gather(g[0, a], a, i, 0, H)
+            xb = interleave(g[0, a], a, 0, H, False)
+            multiply(a, 0, H, *quantise(xb, a, 0, H))
+        gelu(0)
+        for i in range(PACK):
+            gather(g[1, 0], 0, i, H, S)
+        xb = interleave(g[1, 0], 0, H, S, False)
+        multiply(0, H, S, *quantise(xb, 0, H, S))
+        for i in range(PACK - 1):
+            gather(g[1, 1], 1, i, H, S)
+        mid = H + NQ
+        gather(g[1, 1], 1, PACK - 1, H, mid)
+        xb2 = interleave(g[1, 1], 1, H, mid, False)
+        gather(g[1, 1], 1, PACK - 1, mid, S)
+        xb3 = interleave(g[1, 1], 1, mid, S, True)
+        multiply(1, H, mid, *quantise(xb2, 1, H, mid))
+        multiply(1, mid, S, *quantise(xb3, 1, mid, S))
+        scatter(0)
+        gelu(1)
+        scatter(1)
+        nc.sync.dma_start(out=out, in_=out_t[:])

@@ -61,25 +61,21 @@ def tile_list_hboth_gelu_kernel(
         nc.scalar.dma_start(out=wgt_h[0][:], in_=wgt[:, 0:H])
         nc.sync.dma_start(out=planes[0][0][:], in_=x_view[0, 0])
         nc.sync.dma_start(out=wgt_h[1][:], in_=wgt[:, H:S])
-        for n in range(1, 4):
-            nc.sync.dma_start(out=planes[n // PACK][n % PACK][:], in_=x_view[n // PACK, n % PACK])
         for which, scales in enumerate((w4_scales, r8_scales)):
             cols = slice(which * PASSES * P, (which + 1) * PASSES * P)
-            queue = (nc.gpsimd, nc.scalar)[which]
             for q in range(4):
-                queue.dma_start(
+                nc.gpsimd.dma_start(
                     out=sc_t[32 * q : 32 * q + 4, cols].rearrange("r (a n) -> r a n", a=PASSES).bitcast(I32),
                     in_=scales[:, 4 * q : 4 * q + 4, :].rearrange("a r n -> r a n").bitcast(I32),
                 )
-        for n in range(4, PASSES * PACK):
-            if n == 6:
-                nc.sync.dma_start(out=offs2_t[:], in_=offs2)
+        for n in range(1, PASSES * PACK):
             nc.sync.dma_start(out=planes[n // PACK][n % PACK][:], in_=x_view[n // PACK, n % PACK])
-        nc.sync.dma_start(out=b_t[:], in_=b.rearrange("(p o) -> p o", o=1))
+        nc.sync.dma_start(out=w4_t[:].bitcast(I32), in_=w4_words.rearrange("a p n -> p a n").bitcast(I32))
         nc.sync.dma_start(
             out=r8_t[:].bitcast(I32), in_=r8_words.rearrange("a p n i -> p a (n i)").bitcast(I32)
         )
-        nc.sync.dma_start(out=w4_t[:].bitcast(I32), in_=w4_words.rearrange("a p n -> p a n").bitcast(I32))
+        nc.sync.dma_start(out=b_t[:], in_=b.rearrange("(p o) -> p o", o=1))
+        nc.sync.dma_start(out=offs2_t[:], in_=offs2)
         nc.sync.dma_start(out=wgo_t[:], in_=wgo)
 
         acc = [psum.tile([P, NQ], F32, name="acc%d" % q) for q in range(4)]
@@ -152,16 +148,16 @@ def tile_list_hboth_gelu_kernel(
             for h in range(2)
             for a in range(PASSES)
         }
-        for a in range(PASSES):
+        for h in range(2):
             for i in range(PACK):
-                gather(g[0, a], a, i, 0, H)
-            xb = interleave(g[0, a], a, 0, H, False)
-            multiply(a, 0, H, *quantise(xb, a, 0, H))
-        gelu(0)
+                gather(g[h, 0], 0, i, h * H, (h + 1) * H)
+            xb = interleave(g[h, 0], 0, h * H, (h + 1) * H, False)
+            multiply(0, h * H, (h + 1) * H, *quantise(xb, 0, h * H, (h + 1) * H))
         for i in range(PACK):
-            gather(g[1, 0], 0, i, H, S)
-        xb = interleave(g[1, 0], 0, H, S, False)
-        multiply(0, H, S, *quantise(xb, 0, H, S))
+            gather(g[0, 1], 1, i, 0, H)
+        xb = interleave(g[0, 1], 1, 0, H, False)
+        multiply(1, 0, H, *quantise(xb, 1, 0, H))
+        gelu(0)
         for i in range(PACK - 1):
             gather(g[1, 1], 1, i, H, S)
         mid = H + NQ

@@ -57,25 +57,28 @@ def tile_list_hboth_gelu_kernel(
         nc.scalar.activation(warm[:], dummy[:], GELU)
 
         x_view = xT.rearrange("(a p i) t -> a i p t", a=PASSES, p=P, i=PACK)
-        nc.sync.dma_start(out=offs_t[:], in_=offs)
-        nc.scalar.dma_start(out=wgt_h[0][:], in_=wgt[:, 0:H])
         nc.sync.dma_start(out=planes[0][0][:], in_=x_view[0, 0])
+        nc.scalar.dma_start(out=wgt_h[0][:], in_=wgt[:, 0:H])
+        nc.sync.dma_start(out=offs_t[:], in_=offs)
         nc.sync.dma_start(out=wgt_h[1][:], in_=wgt[:, H:S])
+        for n in range(1, 4):
+            nc.sync.dma_start(out=planes[n // PACK][n % PACK][:], in_=x_view[n // PACK, n % PACK])
         for which, scales in enumerate((w4_scales, r8_scales)):
             cols = slice(which * PASSES * P, (which + 1) * PASSES * P)
             for q in range(4):
-                nc.gpsimd.dma_start(
+                nc.scalar.dma_start(
                     out=sc_t[32 * q : 32 * q + 4, cols].rearrange("r (a n) -> r a n", a=PASSES).bitcast(I32),
                     in_=scales[:, 4 * q : 4 * q + 4, :].rearrange("a r n -> r a n").bitcast(I32),
                 )
-        for n in range(1, PASSES * PACK):
+        for n in range(4, PASSES * PACK):
+            if n == 6:
+                nc.sync.dma_start(out=offs2_t[:], in_=offs2)
             nc.sync.dma_start(out=planes[n // PACK][n % PACK][:], in_=x_view[n // PACK, n % PACK])
-        nc.sync.dma_start(out=w4_t[:].bitcast(I32), in_=w4_words.rearrange("a p n -> p a n").bitcast(I32))
+        nc.sync.dma_start(out=b_t[:], in_=b.rearrange("(p o) -> p o", o=1))
         nc.sync.dma_start(
             out=r8_t[:].bitcast(I32), in_=r8_words.rearrange("a p n i -> p a (n i)").bitcast(I32)
         )
-        nc.sync.dma_start(out=b_t[:], in_=b.rearrange("(p o) -> p o", o=1))
-        nc.sync.dma_start(out=offs2_t[:], in_=offs2)
+        nc.sync.dma_start(out=w4_t[:].bitcast(I32), in_=w4_words.rearrange("a p n -> p a n").bitcast(I32))
         nc.sync.dma_start(out=wgo_t[:], in_=wgo)
 
         acc = [psum.tile([P, NQ], F32, name="acc%d" % q) for q in range(4)]
@@ -170,4 +173,5 @@ def tile_list_hboth_gelu_kernel(
         scatter(0)
         gelu(1)
         scatter(1)
-        nc.sync.dma_start(out=out, in_=out_t[:])
+        nc.sync.dma_start(out=out[:, 0:S], in_=out_t[:, 0:S])
+        nc.scalar.dma_start(out=out[:, S:T], in_=out_t[:, S:T])

from contextlib import ExitStack

import concourse.mybir as mybir

FLOPS = 268435456

F32 = mybir.dt.float32
BF16 = mybir.dt.bfloat16
U8 = mybir.dt.uint8
U16 = mybir.dt.uint16
U32 = mybir.dt.uint32
I32 = mybir.dt.int32
E4M3 = mybir.dt.float8_e4m3fn_x4
E2M1 = mybir.dt.float4_e2m1fn_x4

MULT = mybir.AluOpType.mult
COPY = mybir.ActivationFunctionType.Copy
GELU = mybir.ActivationFunctionType.Gelu_apprx_tanh

P = 128
T = 1024
S = 512
H = 256
NQ = 128
PASSES = 2
PACK = 4
OC = H // 16


def tile_list_hboth_gelu_kernel(
    tc, xT, w4_words, w4_scales, r8_words, r8_scales, wgt, b, wgo, offs, offs2, out
):
    nc = tc.nc
    with ExitStack() as ctx:
        keep = ctx.enter_context(tc.tile_pool(name="keep", bufs=1))
        psum = ctx.enter_context(tc.psum_pool(name="psum", bufs=1))

        offs_t = keep.tile([P, S // 16], U16, name="offs_t")
        offs2_t = keep.tile([P, S // 16], U16, name="offs2_t")
        wgt_h = [keep.tile([P, H], F32, name="wgt%d" % h, align_bytes=64) for h in range(2)]
        wgo_t = keep.tile([P, S], F32, name="wgo_t", align_bytes=64)
        b_t = keep.tile([P, 1], F32, name="b_t")
        dummy = keep.tile([P, 1], F32, name="dummy")
        w4_t = keep.tile([P, PASSES, 2 * P], U8, name="w4_t", align_bytes=64)
        r8_t = keep.tile([P, PASSES, P * PACK], U8, name="r8_t", align_bytes=64)
        sc_t = keep.tile([P, 2 * PASSES * P], U8, name="sc_t", align_bytes=64)
        out_t = keep.tile([P, T], F32, name="out_t", align_bytes=64)
        planes = [
            [keep.tile([P, T], F32, name="x%d%d" % (a, i), align_bytes=64) for i in range(PACK)]
            for a in range(PASSES)
        ]

        nc.vector.memset(dummy[:], 0.0)
        nc.vector.memset(sc_t[:].bitcast(I32), 0)
        nc.vector.memset(out_t[:], 0.0)
        warm = keep.tile([P, 1], F32, name="warm")
        nc.scalar.activation(warm[:], dummy[:], GELU)

        x_view = xT.rearrange("(a p i) t -> a i p t", a=PASSES, p=P, i=PACK)
        nc.sync.dma_start(out=planes[0][0][:], in_=x_view[0, 0])
        nc.scalar.dma_start(out=wgt_h[0][:], in_=wgt[:, 0:H])
        nc.sync.dma_start(out=offs_t[:], in_=offs)
        nc.sync.dma_start(out=wgt_h[1][:], in_=wgt[:, H:S])
        for n in range(1, 4):
            nc.sync.dma_start(out=planes[n // PACK][n % PACK][:], in_=x_view[n // PACK, n % PACK])
        for which, scales in enumerate((w4_scales, r8_scales)):
            cols = slice(which * PASSES * P, (which + 1) * PASSES * P)
            for q in range(4):
                nc.scalar.dma_start(
                    out=sc_t[32 * q : 32 * q + 4, cols].rearrange("r (a n) -> r a n", a=PASSES).bitcast(I32),
                    in_=scales[:, 4 * q : 4 * q + 4, :].rearrange("a r n -> r a n").bitcast(I32),
                )
        for n in range(4, PASSES * PACK):
            if n == 6:
                nc.sync.dma_start(out=offs2_t[:], in_=offs2)
            nc.sync.dma_start(out=planes[n // PACK][n % PACK][:], in_=x_view[n // PACK, n % PACK])
        nc.sync.dma_start(out=b_t[:], in_=b.rearrange("(p o) -> p o", o=1))
        nc.sync.dma_start(
            out=r8_t[:].bitcast(I32), in_=r8_words.rearrange("a p n i -> p a (n i)").bitcast(I32)
        )
        nc.sync.dma_start(out=w4_t[:].bitcast(I32), in_=w4_words.rearrange("a p n -> p a n").bitcast(I32))
        nc.sync.dma_start(out=wgo_t[:], in_=wgo)

        acc = [psum.tile([P, NQ], F32, name="acc%d" % q) for q in range(4)]
        val = [keep.tile([P, H], F32, name="val%d" % h, align_bytes=64) for h in range(2)]

        def gather(g, a, i, j0, j1):
            h = j0 // H
            nc.vector.tensor_tensor(
                g[:, i, j0 - h * H : j1 - h * H],
                planes[a][i][:].indirect(offs_t[:, j0 // 16 : j1 // 16]),
                wgt_h[h][:, j0 - h * H : j1 - h * H],
                MULT,
            )

        def interleave(g, a, j0, j1, on_vector):
            h = j0 // H
            xb = keep.tile([P, (j1 - j0) * PACK], BF16, name="xb%d_%d" % (a, j0), align_bytes=64)
            dst = xb[:].rearrange("p (c i t) -> p c t i", i=4, t=PACK)
            src = g[:, :, j0 - h * H : j1 - h * H].rearrange("p t (c i) -> p c t i", i=4)
            if on_vector:
                nc.vector.tensor_copy(dst, src)
            else:
                nc.scalar.activation(dst, src, COPY)
            return xb

        def quantise(xb, a, j0, j1):
            codes = keep.tile([P, j1 - j0], U32, name="codes%d_%d" % (a, j0), align_bytes=64)
            scales = keep.tile([P, j1 - j0], U8, name="scales%d_%d" % (a, j0), align_bytes=64)
            nc.vector.quantize_mx(out=codes[:].bitcast(E4M3), scales=scales[:], in_=xb[:])
            return codes, scales

        def multiply(a, j0, j1, codes, scales):
            for j in range(j0, j1, NQ):
                cols = slice(j - j0, j - j0 + NQ)
                nc.tensor.matmul_mx(
                    out=acc[j // NQ][:],
                    lhsT=w4_t[:, a, :].bitcast(E2M1),
                    lhsT_scale=sc_t[:, a * P : (a + 1) * P],
                    rhs=codes[:, cols].bitcast(E4M3),
                    rhs_scale=scales[:, cols],
                    start=(a == 0),
                    stop=False,
                )
                nc.tensor.matmul_mx(
                    out=acc[j // NQ][:],
                    lhsT=r8_t[:, a, :].bitcast(E4M3),
                    lhsT_scale=sc_t[:, (PASSES + a) * P : (PASSES + a + 1) * P],
                    rhs=codes[:, cols].bitcast(E4M3),
                    rhs_scale=scales[:, cols],
                    start=False,
                    stop=(a == PASSES - 1),
                )

        def gelu(h):
            for s in range(2):
                nc.scalar.activation(
                    val[h][:, s * NQ : (s + 1) * NQ], acc[2 * h + s][:], GELU, bias=b_t[:, 0:1]
                )

        def scatter(h):
            nc.vector.tensor_tensor(
                out_t[:].indirect(offs2_t[:, h * OC : (h + 1) * OC]),
                val[h][:],
                wgo_t[:, h * H : (h + 1) * H],
                MULT,
            )

        g = {
            (h, a): keep.tile([P, PACK, H], F32, name="g%d%d" % (h, a), align_bytes=64)
            for h in range(2)
            for a in range(PASSES)
        }
        for h in range(2):
            for i in range(PACK):
                gather(g[h, 0], 0, i, h * H, (h + 1) * H)
            xb = interleave(g[h, 0], 0, h * H, (h + 1) * H, False)
            multiply(0, h * H, (h + 1) * H, *quantise(xb, 0, h * H, (h + 1) * H))
        for i in range(PACK):
            gather(g[0, 1], 1, i, 0, H)
        xb = interleave(g[0, 1], 1, 0, H, False)
        multiply(1, 0, H, *quantise(xb, 1, 0, H))
        gelu(0)
        for i in range(PACK - 1):
            gather(g[1, 1], 1, i, H, S)
        mid = H + NQ
        gather(g[1, 1], 1, PACK - 1, H, mid)
        xb2 = interleave(g[1, 1], 1, H, mid, False)
        gather(g[1, 1], 1, PACK - 1, mid, S)
        xb3 = interleave(g[1, 1], 1, mid, S, True)
        multiply(1, H, mid, *quantise(xb2, 1, H, mid))
        multiply(1, mid, S, *quantise(xb3, 1, mid, S))
        scatter(0)
        gelu(1)
        scatter(1)
        nc.sync.dma_start(out=out[:, 0:S], in_=out_t[:, 0:S])
        nc.scalar.dma_start(out=out[:, S:T], in_=out_t[:, S:T])
